import numpy as np
import ml_dtypes


def mxq(x, axis, fmt="e4m3"):
    dtype, down = {"e4m3": (ml_dtypes.float8_e4m3fn, 7), "e5m2": (ml_dtypes.float8_e5m2, 14)}[fmt]
    v = np.moveaxis(np.asarray(x, np.float32).astype(ml_dtypes.bfloat16).astype(np.float64), axis, -1)
    blocks = v.reshape(v.shape[:-1] + (-1, 32))
    amax = np.abs(blocks).max(-1, keepdims=True)
    byte = np.maximum(np.where(amax > 0, np.frexp(amax)[1] - 1 + 127, 0) - down, 1)
    scale = np.exp2(byte - 127.0)
    codes = (blocks / scale).astype(np.float32).astype(dtype).astype(np.float64)
    return np.moveaxis((codes * scale).reshape(v.shape), -1, axis)


WIDE = False


def mx_kscale(k):
    if not WIDE:
        return np.ones(k)
    levels = np.array([10, -10, 5, -5, 0])
    if k % 512:
        return np.exp2(np.random.permutation(np.resize(levels, k // 32))).repeat(32)
    a = np.empty((k // 512, 16))
    for p in range(k // 512):
        a[p, :8] = np.random.permutation(np.resize(levels, 8))
        for g in range(8):
            far = levels[np.abs(levels - a[p, g]) >= 10]
            a[p, g + 8] = far[np.random.randint(len(far))]
    return np.exp2(a.ravel()).repeat(32)


BF16 = ml_dtypes.bfloat16


def bf(x):
    return np.asarray(x, np.float32).astype(BF16)


def f64(x):
    return np.asarray(x).astype(np.float64)


E2M1 = np.array([0.0, 0.5, 1.0, 1.5, 2.0, 3.0, 4.0, 6.0, -0.0, -0.5, -1.0, -1.5, -2.0, -3.0, -4.0, -6.0])


def pack_weight(w, fmt):
    k, n = w.shape
    w = f64(bf(w)).reshape(k // 32, 32, n)
    amax = np.abs(w).max(1)
    if fmt == "e4m3":
        byte = np.frexp(amax)[1] - 1 + 127 - 7
    else:
        mant, ex = np.frexp(amax / 6.0)
        byte = np.where(mant > 0.5, ex, ex - 1) + 127
    byte = np.clip(np.where(amax > 0, byte, 1), 1, 254)
    scaled = (w * np.exp2(127.0 - byte)[:, None, :]).reshape(k, n).astype(np.float32)
    by_word = np.ascontiguousarray(scaled.reshape(k // 512, 128, 4, n).transpose(0, 1, 3, 2))
    if fmt == "e4m3":
        words = by_word.astype(ml_dtypes.float8_e4m3fn).view(np.uint8)
    else:
        c = by_word.astype(ml_dtypes.float4_e2m1fn).view(np.uint8) & 0xF
        words = c[..., 0::2] | (c[..., 1::2] << 4)
    return np.ascontiguousarray(words), np.ascontiguousarray(byte.astype(np.uint8).reshape(k // 512, 16, n))


def unpack_weight(words, scales, fmt):
    g, p, n, _ = words.shape
    if fmt == "e4m3":
        vals = np.ascontiguousarray(words).view(ml_dtypes.float8_e4m3fn).astype(np.float64)
    else:
        nib = np.empty((g, p, n, 4), np.uint8)
        nib[..., 0::2] = words & 0xF
        nib[..., 1::2] = words >> 4
        vals = E2M1[nib]
    vals = vals * np.repeat(np.exp2(scales.astype(np.float64) - 127.0), 8, axis=1)[..., None]
    return vals.transpose(0, 1, 3, 2).reshape(g * 512, n)
def pack4(w):
    words, scales = pack_weight(w, "e2m1")
    return words.reshape(words.shape[0], 128, -1), scales


def unpack4(words, scales):
    return unpack_weight(words.reshape(words.shape[0], 128, -1, 2), scales, "e2m1")


def planes(Y):
    n, m = Y.shape
    b = f64(bf(Y)).reshape(n // 32, 32, m)
    amax = np.abs(b).max(1)
    byte = np.clip(np.where(amax > 0, np.frexp(amax)[1] - 1 + 127 - 7, 1), 1, 254)
    codes = (b * np.exp2(127.0 - byte)[:, None, :]).reshape(n, m).astype(np.float32).astype(ml_dtypes.float8_e4m3fn).view(np.uint8)
    words = codes.reshape(n // 512, 128, 4, m).transpose(0, 1, 3, 2)
    return np.ascontiguousarray(words), np.ascontiguousarray(byte.astype(np.uint8).reshape(n // 512, 16, m))


K, R, G = 2048, 1024, 1536

def noise(*shape):
    return np.random.randn(*shape)

def setup_inputs():
    s = mx_kscale(K)
    t = mx_kscale(R)
    row = np.exp(0.8 * noise(R, 1))
    lower = noise(R, K) * row * s[None, :]
    pivot_inv = np.exp(0.4 * noise(K))
    upper = noise(K, R) / np.sqrt(K) / s[:, None] * t[None, :]
    diag = noise(R, R) * row * t[None, :]
    guesses = noise(R, G) / np.sqrt(R) / t[:, None]
    u_words, u_scales = pack4(upper)
    return {"lower": bf(lower), "pivot_inv": bf(pivot_inv), "u_words": u_words, "u_scales": u_scales,
            "diag": bf(diag), "guesses": bf(guesses)}

def reference(lower, pivot_inv, u_words, u_scales, diag, guesses):
    L, D, X = f64(lower), f64(diag), f64(guesses)
    U = unpack4(u_words, u_scales)
    F = -(L * f64(pivot_inv)[None, :])
    S = (mxq(F, 1, "e4m3") @ U) + D
    y = mxq(S, 1, "e4m3") @ mxq(X, 0, "e4m3")
    Y = y
    words, scales = planes(Y)
    return y, words, scales

@@ -1,0 +1,409 @@
+from contextlib import ExitStack
+
+import concourse.mybir as mybir
+from concourse.masks import make_identity
+
+K, R, G = 2048, 1024, 1536
+FLOPS = 2 * R * K * R + 2 * R * R * G
+
+F32 = mybir.dt.float32
+BF16 = mybir.dt.bfloat16
+I32 = mybir.dt.int32
+U32 = mybir.dt.uint32
+U8 = mybir.dt.uint8
+FP8X4 = mybir.dt.float8_e4m3fn_x4
+FP4X4 = mybir.dt.float4_e2m1fn_x4
+ALU = mybir.AluOpType
+
+P = 128
+PASS = 512
+NK = K // PASS
+NC = R // PASS
+NG = G // 512
+PAIRS = 4
+BANKS = 8
+
+
+def tile_schur_complement_apply_h1_kernel(
+    tc, lower, pivot_inv, u_words, u_scales, diag, guesses, out_0, out_1, out_2
+):
+    nc = tc.nc
+    with ExitStack() as ctx:
+        keep = ctx.enter_context(tc.tile_pool(name="keep", bufs=1))
+        psum = ctx.enter_context(tc.psum_pool(name="psum", bufs=1))
+        ctx.enter_context(tc.manual_schedule(engines={mybir.EngineType.PE}))
+
+        free_banks = list(range(BANKS))
+
+        def new_bank(shape):
+            index = free_banks.pop(0)
+            bank = psum.tile(shape, F32, name="bank%d" % index, tag="bank%d" % index)
+            return bank, index
+
+        def pair_rows(matrix, pair):
+            group, half = divmod(pair, 2)
+            rows = matrix[group * PASS : (group + 1) * PASS, :].rearrange("(p t) c -> p t c", t=4)
+            return rows[:, 2 * half : 2 * half + 2, :]
+
+        l_tiles = {}
+
+        def load_lower(pair, g0, g1):
+            t = keep.tile([P, 2, (g1 - g0) * PASS], BF16, name="l_%d_%d" % (pair, g0), align_bytes=64)
+            nc.sync.dma_start(out=t[:], in_=pair_rows(lower, pair)[:, :, g0 * PASS : g1 * PASS])
+            for g in range(g0, g1):
+                l_tiles[pair, g] = (t, g - g0)
+
+        u_tiles = {}
+
+        def load_upper(h):
+            t = keep.tile([P, NK, R], U8, name="u_%d" % h, align_bytes=64)
+            nc.sync.dma_start(
+                out=t[:].bitcast(I32),
+                in_=u_words[:, :, 1024 * h : 1024 * (h + 1)].rearrange("g p n -> p g n").bitcast(I32),
+            )
+            u_tiles[h] = t
+
+        d_tiles = {}
+
+        def load_diag(pair):
+            t = keep.tile([P, 2, R], BF16, name="d_%d" % pair, align_bytes=64)
+            nc.sync.dma_start(out=t[:], in_=pair_rows(diag, pair))
+            d_tiles[pair] = t
+
+        x_tiles = {}
+
+        def load_guesses(h, n):
+            t = keep.tile([P, 4, 512], BF16, name="x_%d_%d" % (h, n), align_bytes=64)
+            rows = guesses[h * PASS : (h + 1) * PASS, 512 * n : 512 * (n + 1)]
+            nc.sync.dma_start(out=t[:], in_=rows.rearrange("(p t) m -> p t m", t=4))
+            x_tiles[h, n] = t
+
+        ident = keep.tile([P, P], F32, name="ident")
+        u_plane = keep.tile([P, NK, R], U8, name="u_plane", align_bytes=64)
+        piv = keep.tile([P, NK, 2, 2], BF16, name="piv", align_bytes=64)
+        neg_piv = keep.tile([P, NK, 2, 2], BF16, name="neg_piv", align_bytes=64)
+        nc.vector.memset(u_plane[:].rearrange("p g n -> p (g n)").bitcast(I32), 0)
+        make_identity(nc, ident[:])
+        load_lower(0, 0, 1)
+        nc.sync.dma_start(
+            out=piv[:].rearrange("p g u e -> p g (u e)"),
+            in_=pivot_inv.rearrange("(g p t) -> p g t", g=NK, t=4),
+        )
+        load_lower(0, 1, 2)
+        load_lower(0, 2, 4)
+        for q in range(4):
+            nc.scalar.dma_start(
+                out=u_plane[32 * q : 32 * q + 4, :, :].bitcast(I32),
+                in_=u_scales[:, 4 * q : 4 * q + 4, :].rearrange("g r n -> r g n").bitcast(I32),
+            )
+        load_upper(0)
+        load_lower(1, 0, 2)
+        load_lower(1, 2, 4)
+        load_upper(1)
+        load_diag(0)
+        load_guesses(0, 0)
+        load_lower(2, 0, 2)
+        load_diag(1)
+        load_guesses(1, 0)
+        load_lower(2, 2, 4)
+        load_guesses(0, 1)
+        load_guesses(1, 1)
+        load_lower(3, 0, 2)
+        load_diag(2)
+        load_lower(3, 2, 4)
+        load_guesses(0, 2)
+        load_guesses(1, 2)
+        load_diag(3)
+        nc.vector.tensor_scalar(
+            out=neg_piv[:].rearrange("p g u e -> p (g u e)"),
+            in0=piv[:].rearrange("p g u e -> p (g u e)"),
+            scalar1=-1.0,
+            scalar2=None,
+            op0=ALU.mult,
+        )
+
+        lt_banks, f_bf, f_mx = {}, {}, {}
+
+        l_sorted = {}
+
+        def sort_lower(pair, g):
+            t, i = l_tiles[pair, g]
+            words = t[:].bitcast(F32)[:, :, 256 * i : 256 * (i + 1)]
+            ls = keep.tile([P, 2, 2, P], F32, name="l_sorted", tag="l_sorted", bufs=4, align_bytes=64)
+            nc.scalar.copy(out=ls[:], in_=words.rearrange("r j (p u) -> r j u p", u=2))
+            l_sorted[pair, g] = ls
+
+        def turn_lower(pair, g):
+            t, i = l_tiles[pair, g]
+            words = t[:].bitcast(F32)
+            bank, index = new_bank([P, 2, 2, P])
+            for j in range(2):
+                for u in range(2):
+                    if (pair, g) in l_sorted:
+                        src = l_sorted[pair, g][:, j, u, :]
+                    else:
+                        src = words[:, j, 256 * i + u : 256 * (i + 1) : 2]
+                    nc.tensor.transpose(bank[:, u, j, :], src, ident[:])
+            lt_banks[pair, g] = bank, index
+
+        def scale_lower(pair, g):
+            fb = keep.tile([P, 2 * P, 2, 2], BF16, name="f_bf", tag="f_bf", bufs=4, align_bytes=64)
+            bank, index = lt_banks[pair, g]
+            free_banks.append(index)
+            src = bank[:].rearrange("p u j r -> p u (j r)").bitcast(BF16)
+            nc.vector.tensor_tensor(
+                out=fb[:],
+                in0=src.rearrange("p u (n e) -> p n u e", e=2),
+                in1=neg_piv[:, g : g + 1, :, :].to_broadcast([P, 2 * P, 2, 2]),
+                op=ALU.mult,
+            )
+            f_bf[pair, g] = fb
+
+        def quantize(src, width, name, bufs):
+            codes = keep.tile([P, width], U32, name=name + "_codes", tag=name + "_codes", bufs=bufs, align_bytes=64)
+            plane = keep.tile([P, width], U8, name=name + "_plane", tag=name + "_plane", bufs=bufs, align_bytes=64)
+            nc.vector.quantize_mx(out=codes[:].bitcast(FP8X4), scales=plane[:], in_=src)
+            return codes, plane
+
+        def quantize_f(pair, g):
+            f_mx[pair, g] = quantize(f_bf[pair, g][:].rearrange("p n u e -> p (n u e)"), 2 * P, "f", 8)
+
+        s_banks, s_bf, st_banks, st_bf, s_mx = {}, {}, {}, {}, {}
+
+        def first_product(pair, halves, passes):
+            for g in passes:
+                codes, plane = f_mx[pair, g]
+                for h in halves:
+                    for j in range(2):
+                        if g == 0:
+                            s_banks[pair, h, j] = new_bank([P, 512])
+                        nc.tensor.matmul_mx(
+                            out=s_banks[pair, h, j][0][:],
+                            lhsT=codes[:, j * P : (j + 1) * P].bitcast(FP8X4),
+                            lhsT_scale=plane[:, j * P : (j + 1) * P],
+                            rhs=u_tiles[h][:, g, :].bitcast(FP4X4),
+                            rhs_scale=u_plane[:, g, 512 * h : 512 * (h + 1)],
+                            start=(g == 0),
+                            stop=(g == NK - 1),
+                        )
+
+        def add_diag(pair, h, j):
+            sb = keep.tile([P, 2, P, 2], BF16, name="s_bf", tag="s_bf", bufs=6, align_bytes=64)
+            bank, index = s_banks[pair, h, j]
+            free_banks.append(index)
+            nc.vector.tensor_tensor(
+                out=sb[:],
+                in0=bank[:].rearrange("r (p u e) -> r u p e", u=2, e=2),
+                in1=d_tiles[pair][:, j, 512 * h : 512 * (h + 1)].rearrange("r (p u e) -> r u p e", u=2, e=2),
+                op=ALU.add,
+            )
+            s_bf[pair, h, j] = sb
+
+        def turn_s(pair, h):
+            bank, index = new_bank([P, 2, 2, P])
+            for j in range(2):
+                words = s_bf[pair, h, j][:].rearrange("r u p e -> r (u p e)").bitcast(F32)
+                for u in range(2):
+                    nc.tensor.transpose(bank[:, u, j, :], words[:, u * P : (u + 1) * P], ident[:])
+            st_banks[pair, h] = bank, index
+
+        def copy_s(pair, h):
+            stb = keep.tile([P, 2 * P, 4], BF16, name="st_bf", tag="st_bf", bufs=2, align_bytes=64)
+            bank, index = st_banks[pair, h]
+            free_banks.append(index)
+            nc.scalar.copy(out=stb[:].bitcast(F32), in_=bank[:].rearrange("p u j r -> p (j r) u"))
+            st_bf[pair, h] = stb
+
+        def quantize_s(pair, h):
+            s_mx[pair, h] = quantize(st_bf[pair, h][:].rearrange("p n t -> p (n t)"), 2 * P, "s", 8)
+
+        x_bf, x_mx = {}, {}
+
+        def group_x(h, n):
+            xb = keep.tile([P, 512, 4], BF16, name="x_bf", tag="x_bf", bufs=3, align_bytes=64)
+            src = x_tiles[h, n][:].rearrange("p t m -> p m t")
+            for m0 in range(0, 512, 256):
+                nc.scalar.copy(out=xb[:, m0 : m0 + 256, :], in_=src[:, m0 : m0 + 256, :])
+            x_bf[h, n] = xb
+
+        def quantize_x(h, n):
+            x_mx[h, n] = quantize(x_bf[h, n][:].rearrange("p m t -> p (m t)"), 512, "x", 6)
+
+        y_banks, y_f32, y_bf = {}, {}, {}
+        y_planes = {}
+
+        def second_product(pair, n):
+            for h in range(NC):
+                s_codes, s_plane = s_mx[pair, h]
+                x_codes, x_plane = x_mx[h, n]
+                for j in range(2):
+                    if h == 0:
+                        y_banks[pair, n, j] = new_bank([P, 512])
+                    nc.tensor.matmul_mx(
+                        out=y_banks[pair, n, j][0][:],
+                        lhsT=s_codes[:, j * P : (j + 1) * P].bitcast(FP8X4),
+                        lhsT_scale=s_plane[:, j * P : (j + 1) * P],
+                        rhs=x_codes[:].bitcast(FP8X4),
+                        rhs_scale=x_plane[:],
+                        start=(h == 0),
+                        stop=(h == NC - 1),
+                    )
+
+        def copy_y(pair, n):
+            group, half = divmod(pair, 2)
+            if half == 0:
+                y_f32[group, n] = keep.tile([P, 4, 512], F32, name="y_%d_%d" % (group, n), align_bytes=64)
+            yt = y_f32[group, n]
+            for j in range(2):
+                bank, index = y_banks[pair, n, j]
+                free_banks.append(index)
+                nc.scalar.copy(out=yt[:, 2 * half + j, :], in_=bank[:])
+            nc.sync.dma_start(
+                out=pair_rows(out_0, pair)[:, :, 512 * n : 512 * (n + 1)], in_=yt[:, 2 * half : 2 * half + 2, :]
+            )
+
+        def group_y(group, n, split=512):
+            yb = keep.tile([P, 512, 4], BF16, name="y_bf", tag="y_bf", bufs=2, align_bytes=64)
+            src = y_f32[group, n][:].rearrange("p t m -> p m t")
+            nc.vector.tensor_copy(out=yb[:, :split, :], in_=src[:, :split, :])
+            if split < 512:
+                nc.scalar.copy(out=yb[:, split:, :], in_=src[:, split:, :])
+            y_bf[group, n] = yb
+
+        def quantize_y(group, n):
+            if n == 0:
+                y_planes[group] = keep.tile([P, G], U8, name="y_plane_%d" % group, align_bytes=64)
+            plane = y_planes[group]
+            codes = keep.tile([P, 512], U32, name="y_codes_%d_%d" % (group, n), align_bytes=64)
+            nc.vector.quantize_mx(
+                out=codes[:].bitcast(FP8X4),
+                scales=plane[:, 512 * n : 512 * (n + 1)],
+                in_=y_bf[group, n][:].rearrange("p m t -> p (m t)"),
+            )
+            nc.sync.dma_start(
+                out=out_1[group, :, 512 * n : 512 * (n + 1), :].rearrange("p m t -> p (m t)").bitcast(I32),
+                in_=codes[:].bitcast(I32),
+            )
+            if n == NG - 1:
+                for q in range(4):
+                    queue = nc.sync if q % 2 == 0 or group == 0 else nc.scalar
+                    queue.dma_start(
+                        out=out_2[group, 4 * q : 4 * q + 4, :].bitcast(I32),
+                        in_=plane[32 * q : 32 * q + 4, :].bitcast(I32),
+                    )
+
+        def make_f(pair, passes):
+            for g in passes:
+                scale_lower(pair, g)
+                if g > passes[0]:
+                    quantize_f(pair, g - 1)
+
+        def product_y(*units):
+            for unit in units:
+                second_product(*unit)
+                copy_y(*unit)
+
+        def add_half(pair, h):
+            add_diag(pair, h, 0)
+            add_diag(pair, h, 1)
+
+        for g in range(NK):
+            turn_lower(0, g)
+        make_f(0, (0, 1, 2, 3))
+        quantize_f(0, 3)
+        for g in range(NK):
+            sort_lower(1, g)
+        first_product(0, (0,), range(NK))
+        for g in range(NK):
+            turn_lower(1, g)
+        make_f(1, (0, 1, 2, 3))
+        group_x(0, 0)
+        first_product(0, (1,), range(NK))
+        add_diag(0, 0, 0)
+        quantize_f(1, 3)
+        add_diag(0, 0, 1)
+        add_half(0, 1)
+        first_product(1, (0,), range(NK))
+        turn_s(0, 0)
+        turn_s(0, 1)
+        turn_lower(2, 0)
+        turn_lower(2, 1)
+        copy_s(0, 0)
+        copy_s(0, 1)
+        group_x(1, 0)
+        add_half(1, 0)
+        make_f(2, (0, 1))
+        quantize_s(0, 0)
+        quantize_f(2, 1)
+        quantize_s(0, 1)
+        quantize_x(0, 0)
+        first_product(1, (1,), range(NK))
+        turn_s(1, 0)
+        turn_lower(2, 2)
+        turn_lower(2, 3)
+        quantize_x(1, 0)
+        copy_s(1, 0)
+        group_x(0, 1)
+        add_half(1, 1)
+        make_f(2, (2, 3))
+        quantize_s(1, 0)
+        quantize_f(2, 3)
+        product_y((0, 0))
+        group_x(1, 1)
+        quantize_x(0, 1)
+        first_product(2, (0,), range(NK))
+        turn_s(1, 1)
+        turn_lower(3, 0)
+        turn_lower(3, 1)
+        copy_s(1, 1)
+        add_half(2, 0)
+        quantize_x(1, 1)
+        make_f(3, (0, 1))
+        quantize_s(1, 1)
+        quantize_f(3, 1)
+        product_y((0, 1))
+        group_x(0, 2)
+        first_product(2, (1,), range(NK))
+        turn_s(2, 0)
+        turn_lower(3, 2)
+        turn_lower(3, 3)
+        copy_s(2, 0)
+        group_x(1, 2)
+        add_half(2, 1)
+        make_f(3, (2, 3))
+        quantize_x(0, 2)
+        quantize_f(3, 3)
+        quantize_s(2, 0)
+        product_y((1, 0), (1, 1))
+        quantize_x(1, 2)
+        group_y(0, 0)
+        first_product(3, (0,), range(NK))
+        turn_s(2, 1)
+        copy_s(2, 1)
+        group_y(0, 1)
+        quantize_y(0, 0)
+        add_half(3, 0)
+        quantize_s(2, 1)
+        quantize_y(0, 1)
+        product_y((0, 2), (1, 2))
+        first_product(3, (1,), range(NK))
+        turn_s(3, 0)
+        copy_s(3, 0)
+        group_y(0, 2)
+        add_half(3, 1)
+        quantize_s(3, 0)
+        second_product(2, 0)
+        turn_s(3, 1)
+        copy_s(3, 1)
+        copy_y(2, 0)
+        quantize_y(0, 2)
+        quantize_s(3, 1)
+        product_y((2, 1), (3, 0))
+        group_y(1, 0)
+        product_y((3, 1))
+        group_y(1, 1)
+        quantize_y(1, 0)
+        product_y((2, 2), (3, 2))
+        quantize_y(1, 1)
+        group_y(1, 2, 256)
+        quantize_y(1, 2)

@@ -72,11 +72,12 @@ def tile_schur_complement_apply_h1_kernel(
 
         x_tiles = {}
 
-        def load_guesses(h, n):
-            t = keep.tile([P, 4, 512], BF16, name="x_%d_%d" % (h, n), align_bytes=64)
-            rows = guesses[h * PASS : (h + 1) * PASS, 512 * n : 512 * (n + 1)]
+        def load_guesses(h, n0, n1):
+            t = keep.tile([P, 4, 512 * (n1 - n0)], BF16, name="x_%d_%d" % (h, n0), align_bytes=64)
+            rows = guesses[h * PASS : (h + 1) * PASS, 512 * n0 : 512 * n1]
             nc.sync.dma_start(out=t[:], in_=rows.rearrange("(p t) m -> p t m", t=4))
-            x_tiles[h, n] = t
+            for n in range(n0, n1):
+                x_tiles[h, n] = t[:, :, 512 * (n - n0) : 512 * (n - n0 + 1)]
 
         ident = keep.tile([P, P], F32, name="ident")
         u_plane = keep.tile([P, NK, R], U8, name="u_plane", align_bytes=64)
@@ -101,18 +102,15 @@ def tile_schur_complement_apply_h1_kernel(
         load_lower(1, 2, 4)
         load_upper(1)
         load_diag(0)
-        load_guesses(0, 0)
         load_lower(2, 0, 2)
+        load_guesses(0, 0, 1)
         load_diag(1)
-        load_guesses(1, 0)
+        load_guesses(1, 0, 1)
         load_lower(2, 2, 4)
-        load_guesses(0, 1)
-        load_guesses(1, 1)
-        load_lower(3, 0, 2)
+        load_guesses(0, 1, 3)
+        load_lower(3, 0, 4)
         load_diag(2)
-        load_lower(3, 2, 4)
-        load_guesses(0, 2)
-        load_guesses(1, 2)
+        load_guesses(1, 1, 3)
         load_diag(3)
         nc.vector.tensor_scalar(
             out=neg_piv[:].rearrange("p g u e -> p (g u e)"),
@@ -170,11 +168,14 @@ def tile_schur_complement_apply_h1_kernel(
 
         s_banks, s_bf, st_banks, st_bf, s_mx = {}, {}, {}, {}, {}
 
-        def first_product(pair, halves, passes):
-            for g in passes:
+        def first_product(pair, halves, passes, by_tile=False):
+            steps = [(g, j) for g in passes for j in range(2)]
+            if by_tile:
+                steps = [(g, j) for j in range(2) for g in passes]
+            for g, j in steps:
                 codes, plane = f_mx[pair, g]
                 for h in halves:
-                    for j in range(2):
+                    if True:
                         if g == 0:
                             s_banks[pair, h, j] = new_bank([P, 512])
                         nc.tensor.matmul_mx(
@@ -217,13 +218,18 @@ def tile_schur_complement_apply_h1_kernel(
         def quantize_s(pair, h):
             s_mx[pair, h] = quantize(st_bf[pair, h][:].rearrange("p n t -> p (n t)"), 2 * P, "s", 8)
 
+        def interleave(copy, dst, src):
+            copy(
+                out=dst.rearrange("p (c i) t -> p c t i", i=4),
+                in_=src.rearrange("p t (c i) -> p c t i", i=4),
+            )
+
         x_bf, x_mx = {}, {}
 
         def group_x(h, n):
             xb = keep.tile([P, 512, 4], BF16, name="x_bf", tag="x_bf", bufs=3, align_bytes=64)
-            src = x_tiles[h, n][:].rearrange("p t m -> p m t")
             for m0 in range(0, 512, 256):
-                nc.scalar.copy(out=xb[:, m0 : m0 + 256, :], in_=src[:, m0 : m0 + 256, :])
+                interleave(nc.scalar.copy, xb[:, m0 : m0 + 256, :], x_tiles[h, n][:, :, m0 : m0 + 256])
             x_bf[h, n] = xb
 
         def quantize_x(h, n):
@@ -258,16 +264,22 @@ def tile_schur_complement_apply_h1_kernel(
                 bank, index = y_banks[pair, n, j]
                 free_banks.append(index)
                 nc.scalar.copy(out=yt[:, 2 * half + j, :], in_=bank[:])
-            nc.sync.dma_start(
-                out=pair_rows(out_0, pair)[:, :, 512 * n : 512 * (n + 1)], in_=yt[:, 2 * half : 2 * half + 2, :]
-            )
+                if group == 1:
+                    nc.sync.dma_start(
+                        out=pair_rows(out_0, pair)[:, j, 512 * n : 512 * (n + 1)], in_=yt[:, 2 * half + j, :]
+                    )
+            if group == 0:
+                nc.sync.dma_start(
+                    out=pair_rows(out_0, pair)[:, :, 512 * n : 512 * (n + 1)], in_=yt[:, 2 * half : 2 * half + 2, :]
+                )
 
         def group_y(group, n, split=512):
             yb = keep.tile([P, 512, 4], BF16, name="y_bf", tag="y_bf", bufs=2, align_bytes=64)
-            src = y_f32[group, n][:].rearrange("p t m -> p m t")
-            nc.vector.tensor_copy(out=yb[:, :split, :], in_=src[:, :split, :])
+            src = y_f32[group, n]
+            if split > 0:
+                interleave(nc.vector.tensor_copy, yb[:, :split, :], src[:, :, :split])
             if split < 512:
-                nc.scalar.copy(out=yb[:, split:, :], in_=src[:, split:, :])
+                interleave(nc.scalar.copy, yb[:, split:, :], src[:, :, split:])
             y_bf[group, n] = yb
 
         def quantize_y(group, n):
@@ -317,12 +329,14 @@ def tile_schur_complement_apply_h1_kernel(
         for g in range(NK):
             turn_lower(1, g)
         make_f(1, (0, 1, 2, 3))
-        group_x(0, 0)
+        sort_lower(2, 0)
+        sort_lower(2, 1)
         first_product(0, (1,), range(NK))
         add_diag(0, 0, 0)
         quantize_f(1, 3)
         add_diag(0, 0, 1)
         add_half(0, 1)
+        group_x(0, 0)
         first_product(1, (0,), range(NK))
         turn_s(0, 0)
         turn_s(0, 1)
@@ -341,69 +355,71 @@ def tile_schur_complement_apply_h1_kernel(
         turn_s(1, 0)
         turn_lower(2, 2)
         turn_lower(2, 3)
-        quantize_x(1, 0)
         copy_s(1, 0)
-        group_x(0, 1)
-        add_half(1, 1)
+        quantize_x(1, 0)
         make_f(2, (2, 3))
-        quantize_s(1, 0)
         quantize_f(2, 3)
+        add_half(1, 1)
+        quantize_s(1, 0)
         product_y((0, 0))
-        group_x(1, 1)
-        quantize_x(0, 1)
+        group_x(0, 1)
+
         first_product(2, (0,), range(NK))
         turn_s(1, 1)
         turn_lower(3, 0)
         turn_lower(3, 1)
         copy_s(1, 1)
+        group_x(1, 1)
+
         add_half(2, 0)
-        quantize_x(1, 1)
-        make_f(3, (0, 1))
         quantize_s(1, 1)
+        make_f(3, (0, 1))
+        quantize_x(0, 1)
         quantize_f(3, 1)
-        product_y((0, 1))
-        group_x(0, 2)
         first_product(2, (1,), range(NK))
+        quantize_x(1, 1)
+        add_half(2, 1)
+        product_y((1, 0))
         turn_s(2, 0)
+        turn_s(2, 1)
         turn_lower(3, 2)
         turn_lower(3, 3)
-        copy_s(2, 0)
-        group_x(1, 2)
-        add_half(2, 1)
         make_f(3, (2, 3))
-        quantize_x(0, 2)
+        copy_s(2, 0)
+        copy_s(2, 1)
         quantize_f(3, 3)
+        group_x(0, 2)
+        group_x(1, 2)
+        product_y((0, 1), (1, 1))
         quantize_s(2, 0)
-        product_y((1, 0), (1, 1))
+        quantize_s(2, 1)
+        quantize_x(0, 2)
         quantize_x(1, 2)
         group_y(0, 0)
         first_product(3, (0,), range(NK))
-        turn_s(2, 1)
-        copy_s(2, 1)
-        group_y(0, 1)
-        quantize_y(0, 0)
         add_half(3, 0)
-        quantize_s(2, 1)
-        quantize_y(0, 1)
+        quantize_y(0, 0)
+        group_y(0, 1)
         product_y((0, 2), (1, 2))
-        first_product(3, (1,), range(NK))
+        quantize_y(0, 1)
+        first_product(3, (1,), range(NK), by_tile=True)
         turn_s(3, 0)
         copy_s(3, 0)
-        group_y(0, 2)
         add_half(3, 1)
         quantize_s(3, 0)
+        group_y(0, 2)
         second_product(2, 0)
         turn_s(3, 1)
         copy_s(3, 1)
+        quantize_s(3, 1)
         copy_y(2, 0)
         quantize_y(0, 2)
-        quantize_s(3, 1)
         product_y((2, 1), (3, 0))
         group_y(1, 0)
         product_y((3, 1))
-        group_y(1, 1)
         quantize_y(1, 0)
+        group_y(1, 1)
         product_y((2, 2), (3, 2))
         quantize_y(1, 1)
-        group_y(1, 2, 256)
+        group_y(1, 2, 320)
         quantize_y(1, 2)

@@ -31,7 +31,7 @@ def tile_schur_complement_apply_h1_kernel(
     with ExitStack() as ctx:
         keep = ctx.enter_context(tc.tile_pool(name="keep", bufs=1))
         psum = ctx.enter_context(tc.psum_pool(name="psum", bufs=1))
-        ctx.enter_context(tc.manual_schedule(engines={mybir.EngineType.PE}))
+        ctx.enter_context(tc.manual_schedule())
 
         free_banks = list(range(BANKS))
 
@@ -93,7 +93,7 @@ def tile_schur_complement_apply_h1_kernel(
         load_lower(0, 1, 2)
         load_lower(0, 2, 4)
         for q in range(4):
-            nc.scalar.dma_start(
+            nc.sync.dma_start(
                 out=u_plane[32 * q : 32 * q + 4, :, :].bitcast(I32),
                 in_=u_scales[:, 4 * q : 4 * q + 4, :].rearrange("g r n -> r g n").bitcast(I32),
             )
@@ -102,15 +102,16 @@ def tile_schur_complement_apply_h1_kernel(
         load_lower(1, 2, 4)
         load_upper(1)
         load_diag(0)
-        load_lower(2, 0, 2)
         load_guesses(0, 0, 1)
-        load_diag(1)
+        load_lower(2, 0, 2)
         load_guesses(1, 0, 1)
+        load_diag(1)
         load_lower(2, 2, 4)
         load_guesses(0, 1, 3)
-        load_lower(3, 0, 4)
-        load_diag(2)
         load_guesses(1, 1, 3)
+        load_lower(3, 0, 2)
+        load_diag(2)
+        load_lower(3, 2, 4)
         load_diag(3)
         nc.vector.tensor_scalar(
             out=neg_piv[:].rearrange("p g u e -> p (g u e)"),
@@ -119,6 +120,7 @@ def tile_schur_complement_apply_h1_kernel(
             scalar2=None,
             op0=ALU.mult,
         )
+
 
         lt_banks, f_bf, f_mx = {}, {}, {}
 
@@ -145,17 +147,20 @@ def tile_schur_complement_apply_h1_kernel(
             lt_banks[pair, g] = bank, index
 
         def scale_lower(pair, g):
-            fb = keep.tile([P, 2 * P, 2, 2], BF16, name="f_bf", tag="f_bf", bufs=4, align_bytes=64)
+            if g % 2 == 0:
+                f_bf[pair, g // 2] = keep.tile(
+                    [P, 2, 2 * P, 2, 2], BF16, name="f_bf", tag="f_bf", bufs=2, align_bytes=64
+                )
+            fb = f_bf[pair, g // 2][:, g % 2]
             bank, index = lt_banks[pair, g]
             free_banks.append(index)
             src = bank[:].rearrange("p u j r -> p u (j r)").bitcast(BF16)
             nc.vector.tensor_tensor(
-                out=fb[:],
+                out=fb,
                 in0=src.rearrange("p u (n e) -> p n u e", e=2),
                 in1=neg_piv[:, g : g + 1, :, :].to_broadcast([P, 2 * P, 2, 2]),
                 op=ALU.mult,
             )
-            f_bf[pair, g] = fb
 
         def quantize(src, width, name, bufs):
             codes = keep.tile([P, width], U32, name=name + "_codes", tag=name + "_codes", bufs=bufs, align_bytes=64)
@@ -163,8 +168,22 @@ def tile_schur_complement_apply_h1_kernel(
             nc.vector.quantize_mx(out=codes[:].bitcast(FP8X4), scales=plane[:], in_=src)
             return codes, plane
 
-        def quantize_f(pair, g):
-            f_mx[pair, g] = quantize(f_bf[pair, g][:].rearrange("p n u e -> p (n u e)"), 2 * P, "f", 8)
+        f_codes = {}
+
+        def quantize_f(pair, g0, g1):
+            if g0 % 2 == 0:
+                codes = keep.tile([P, 2, 2 * P], U32, name="f_codes", tag="f_codes", bufs=4, align_bytes=64)
+                plane = keep.tile([P, 2, 2 * P], U8, name="f_plane", tag="f_plane", bufs=4, align_bytes=64)
+                f_codes[pair, g0 // 2] = codes, plane
+            codes, plane = f_codes[pair, g0 // 2]
+            part = slice(g0 % 2, g0 % 2 + g1 - g0)
+            nc.vector.quantize_mx(
+                out=codes[:, part].rearrange("p g n -> p (g n)").bitcast(FP8X4),
+                scales=plane[:, part].rearrange("p g n -> p (g n)"),
+                in_=f_bf[pair, g0 // 2][:, part].rearrange("p g n u e -> p (g n u e)"),
+            )
+            for g in range(g0, g1):
+                f_mx[pair, g] = codes[:, g % 2], plane[:, g % 2]
 
         s_banks, s_bf, st_banks, st_bf, s_mx = {}, {}, {}, {}, {}
 
@@ -208,11 +227,11 @@ def tile_schur_complement_apply_h1_kernel(
                     nc.tensor.transpose(bank[:, u, j, :], words[:, u * P : (u + 1) * P], ident[:])
             st_banks[pair, h] = bank, index
 
-        def copy_s(pair, h):
+        def copy_s(pair, h, copy=nc.scalar.copy):
             stb = keep.tile([P, 2 * P, 4], BF16, name="st_bf", tag="st_bf", bufs=2, align_bytes=64)
             bank, index = st_banks[pair, h]
             free_banks.append(index)
-            nc.scalar.copy(out=stb[:].bitcast(F32), in_=bank[:].rearrange("p u j r -> p (j r) u"))
+            copy(out=stb[:].bitcast(F32), in_=bank[:].rearrange("p u j r -> p (j r) u"))
             st_bf[pair, h] = stb
 
         def quantize_s(pair, h):
@@ -236,7 +255,7 @@ def tile_schur_complement_apply_h1_kernel(
             x_mx[h, n] = quantize(x_bf[h, n][:].rearrange("p m t -> p (m t)"), 512, "x", 6)
 
         y_banks, y_f32, y_bf = {}, {}, {}
-        y_planes = {}
+        y_planes, y_codes = {}, {}
 
         def second_product(pair, n):
             for h in range(NC):
@@ -255,7 +274,7 @@ def tile_schur_complement_apply_h1_kernel(
                         stop=(h == NC - 1),
                     )
 
-        def copy_y(pair, n):
+        def copy_y(pair, n, copies=(nc.scalar.copy, nc.scalar.copy)):
             group, half = divmod(pair, 2)
             if half == 0:
                 y_f32[group, n] = keep.tile([P, 4, 512], F32, name="y_%d_%d" % (group, n), align_bytes=64)
@@ -263,23 +282,19 @@ def tile_schur_complement_apply_h1_kernel(
             for j in range(2):
                 bank, index = y_banks[pair, n, j]
                 free_banks.append(index)
-                nc.scalar.copy(out=yt[:, 2 * half + j, :], in_=bank[:])
-                if group == 1:
-                    nc.sync.dma_start(
-                        out=pair_rows(out_0, pair)[:, j, 512 * n : 512 * (n + 1)], in_=yt[:, 2 * half + j, :]
-                    )
-            if group == 0:
-                nc.sync.dma_start(
-                    out=pair_rows(out_0, pair)[:, :, 512 * n : 512 * (n + 1)], in_=yt[:, 2 * half : 2 * half + 2, :]
-                )
+                copies[j](out=yt[:, 2 * half + j, :], in_=bank[:])
+            nc.sync.dma_start(
+                out=pair_rows(out_0, pair)[:, :, 512 * n : 512 * (n + 1)], in_=yt[:, 2 * half : 2 * half + 2, :]
+            )
 
         def group_y(group, n, split=512):
             yb = keep.tile([P, 512, 4], BF16, name="y_bf", tag="y_bf", bufs=2, align_bytes=64)
             src = y_f32[group, n]
             if split > 0:
                 interleave(nc.vector.tensor_copy, yb[:, :split, :], src[:, :, :split])
-            if split < 512:
-                interleave(nc.scalar.copy, yb[:, split:, :], src[:, :, split:])
+            for m0 in range(split, 512, 256):
+                m1 = min(m0 + 256, 512)
+                interleave(nc.scalar.copy, yb[:, m0:m1, :], src[:, :, m0:m1])
             y_bf[group, n] = yb
 
         def quantize_y(group, n):
@@ -292,9 +307,13 @@ def tile_schur_complement_apply_h1_kernel(
                 scales=plane[:, 512 * n : 512 * (n + 1)],
                 in_=y_bf[group, n][:].rearrange("p m t -> p (m t)"),
             )
+            y_codes[group, n] = codes
+
+        def store_planes(group, n):
+            plane = y_planes[group]
             nc.sync.dma_start(
                 out=out_1[group, :, 512 * n : 512 * (n + 1), :].rearrange("p m t -> p (m t)").bitcast(I32),
-                in_=codes[:].bitcast(I32),
+                in_=y_codes[group, n][:].bitcast(I32),
             )
             if n == NG - 1:
                 for q in range(4):
@@ -304,11 +323,9 @@ def tile_schur_complement_apply_h1_kernel(
                         in_=plane[32 * q : 32 * q + 4, :].bitcast(I32),
                     )
 
-        def make_f(pair, passes):
-            for g in passes:
-                scale_lower(pair, g)
-                if g > passes[0]:
-                    quantize_f(pair, g - 1)
+        def make_f(pair, g0):
+            scale_lower(pair, g0)
+            scale_lower(pair, g0 + 1)
 
         def product_y(*units):
             for unit in units:
@@ -319,24 +336,36 @@ def tile_schur_complement_apply_h1_kernel(
             add_diag(pair, h, 0)
             add_diag(pair, h, 1)
 
-        for g in range(NK):
-            turn_lower(0, g)
-        make_f(0, (0, 1, 2, 3))
-        quantize_f(0, 3)
+        turn_lower(0, 0)
+        scale_lower(0, 0)
+        turn_lower(0, 1)
+        scale_lower(0, 1)
+        quantize_f(0, 0, 1)
+        turn_lower(0, 2)
+        turn_lower(0, 3)
+        quantize_f(0, 1, 2)
+        make_f(0, 2)
+        quantize_f(0, 2, 3)
+        quantize_f(0, 3, 4)
         for g in range(NK):
             sort_lower(1, g)
         first_product(0, (0,), range(NK))
         for g in range(NK):
             turn_lower(1, g)
-        make_f(1, (0, 1, 2, 3))
+        make_f(1, 0)
+        scale_lower(1, 2)
+        quantize_f(1, 0, 2)
+        scale_lower(1, 3)
+        group_x(0, 0)
         sort_lower(2, 0)
         sort_lower(2, 1)
+        group_x(1, 0)
         first_product(0, (1,), range(NK))
         add_diag(0, 0, 0)
-        quantize_f(1, 3)
+        quantize_f(1, 2, 4)
         add_diag(0, 0, 1)
         add_half(0, 1)
-        group_x(0, 0)
+        quantize_x(0, 0)
         first_product(1, (0,), range(NK))
         turn_s(0, 0)
         turn_s(0, 1)
@@ -344,82 +373,90 @@ def tile_schur_complement_apply_h1_kernel(
         turn_lower(2, 1)
         copy_s(0, 0)
         copy_s(0, 1)
-        group_x(1, 0)
+        group_x(0, 1)
         add_half(1, 0)
-        make_f(2, (0, 1))
+        make_f(2, 0)
         quantize_s(0, 0)
-        quantize_f(2, 1)
+        quantize_f(2, 0, 2)
         quantize_s(0, 1)
-        quantize_x(0, 0)
+        quantize_x(1, 0)
         first_product(1, (1,), range(NK))
         turn_s(1, 0)
         turn_lower(2, 2)
         turn_lower(2, 3)
         copy_s(1, 0)
-        quantize_x(1, 0)
-        make_f(2, (2, 3))
-        quantize_f(2, 3)
-        add_half(1, 1)
+        group_x(1, 1)
+        make_f(2, 2)
+        add_diag(1, 1, 0)
+        quantize_f(2, 2, 4)
+        add_diag(1, 1, 1)
         quantize_s(1, 0)
         product_y((0, 0))
-        group_x(0, 1)
-
+        quantize_x(0, 1)
         first_product(2, (0,), range(NK))
         turn_s(1, 1)
         turn_lower(3, 0)
         turn_lower(3, 1)
         copy_s(1, 1)
-        group_x(1, 1)
-
+        quantize_x(1, 1)
+        group_x(0, 2)
         add_half(2, 0)
         quantize_s(1, 1)
-        make_f(3, (0, 1))
-        quantize_x(0, 1)
-        quantize_f(3, 1)
+        make_f(3, 0)
+        product_y((0, 1))
+        quantize_f(3, 0, 2)
+        quantize_x(0, 2)
         first_product(2, (1,), range(NK))
-        quantize_x(1, 1)
-        add_half(2, 1)
-        product_y((1, 0))
         turn_s(2, 0)
-        turn_s(2, 1)
         turn_lower(3, 2)
         turn_lower(3, 3)
-        make_f(3, (2, 3))
         copy_s(2, 0)
-        copy_s(2, 1)
-        quantize_f(3, 3)
-        group_x(0, 2)
         group_x(1, 2)
-        product_y((0, 1), (1, 1))
+        add_diag(2, 1, 0)
+        make_f(3, 2)
+        add_diag(2, 1, 1)
+        quantize_f(3, 2, 4)
+        product_y((1, 0), (1, 1))
         quantize_s(2, 0)
-        quantize_s(2, 1)
-        quantize_x(0, 2)
         quantize_x(1, 2)
-        group_y(0, 0)
+        group_y(0, 0, 512)
         first_product(3, (0,), range(NK))
+        turn_s(2, 1)
+        copy_s(2, 1)
+        group_y(0, 1, 512)
         add_half(3, 0)
         quantize_y(0, 0)
-        group_y(0, 1)
+        quantize_s(2, 1)
+        store_planes(0, 0)
         product_y((0, 2), (1, 2))
         quantize_y(0, 1)
+        store_planes(0, 1)
         first_product(3, (1,), range(NK), by_tile=True)
+        group_y(0, 2, 256)
         turn_s(3, 0)
-        copy_s(3, 0)
         add_half(3, 1)
+        copy_s(3, 0)
+        quantize_y(0, 2)
         quantize_s(3, 0)
-        group_y(0, 2)
         second_product(2, 0)
         turn_s(3, 1)
-        copy_s(3, 1)
-        quantize_s(3, 1)
+        store_planes(0, 2)
         copy_y(2, 0)
-        quantize_y(0, 2)
-        product_y((2, 1), (3, 0))
+        copy_s(3, 1, nc.vector.tensor_copy)
+        quantize_s(3, 1)
+        second_product(2, 1)
+        copy_y(2, 1, (nc.scalar.copy, nc.vector.tensor_copy))
+        product_y((3, 0))
         group_y(1, 0)
         product_y((3, 1))
-        quantize_y(1, 0)
         group_y(1, 1)
-        product_y((2, 2), (3, 2))
+        quantize_y(1, 0)
+        product_y((2, 2))
+        second_product(3, 2)
         quantize_y(1, 1)
+        store_planes(1, 0)
+        copy_y(3, 2, (nc.scalar.copy, nc.scalar.copy))
+        store_planes(1, 1)
         group_y(1, 2, 320)
         quantize_y(1, 2)
+        store_planes(1, 2)

@@ -83,7 +83,12 @@ def tile_schur_complement_apply_h1_kernel(
         u_plane = keep.tile([P, NK, R], U8, name="u_plane", align_bytes=64)
         piv = keep.tile([P, NK, 2, 2], BF16, name="piv", align_bytes=64)
         neg_piv = keep.tile([P, NK, 2, 2], BF16, name="neg_piv", align_bytes=64)
+        warm_bf = keep.tile([P, 1024], BF16, name="warm_bf", align_bytes=64)
+        warm_codes = keep.tile([P, 256], U32, name="warm_codes", align_bytes=64)
+        warm_plane = keep.tile([P, 256], U8, name="warm_plane", align_bytes=64)
+        nc.gpsimd.memset(warm_bf[:].bitcast(I32), 0)
         nc.vector.memset(u_plane[:].rearrange("p g n -> p (g n)").bitcast(I32), 0)
+        nc.vector.quantize_mx(out=warm_codes[:].bitcast(FP8X4), scales=warm_plane[:], in_=warm_bf[:])
         make_identity(nc, ident[:])
         load_lower(0, 0, 1)
         nc.sync.dma_start(
@@ -121,6 +126,20 @@ def tile_schur_complement_apply_h1_kernel(
             op0=ALU.mult,
         )
 
+
+        def warm(count):
+            bank, index = new_bank([P, 256])
+            free_banks.append(index)
+            for i in range(count):
+                nc.tensor.matmul_mx(
+                    out=bank[:],
+                    lhsT=warm_codes[:, :P].bitcast(FP8X4),
+                    lhsT_scale=warm_plane[:, :P],
+                    rhs=warm_codes[:].bitcast(FP8X4),
+                    rhs_scale=warm_plane[:],
+                    start=True,
+                    stop=True,
+                )
 
         lt_banks, f_bf, f_mx = {}, {}, {}
 
@@ -336,11 +355,13 @@ def tile_schur_complement_apply_h1_kernel(
             add_diag(pair, h, 0)
             add_diag(pair, h, 1)
 
+        warm(8)
         turn_lower(0, 0)
         scale_lower(0, 0)
         turn_lower(0, 1)
         scale_lower(0, 1)
         quantize_f(0, 0, 1)
+        warm(4)
         turn_lower(0, 2)
         turn_lower(0, 3)
         quantize_f(0, 1, 2)

from contextlib import ExitStack

import concourse.mybir as mybir
from concourse.masks import make_identity

K, R, G = 2048, 1024, 1536
FLOPS = 2 * R * K * R + 2 * R * R * G

F32 = mybir.dt.float32
BF16 = mybir.dt.bfloat16
I32 = mybir.dt.int32
U32 = mybir.dt.uint32
U8 = mybir.dt.uint8
FP8X4 = mybir.dt.float8_e4m3fn_x4
FP4X4 = mybir.dt.float4_e2m1fn_x4
ALU = mybir.AluOpType

P = 128
PASS = 512
NK = K // PASS
NC = R // PASS
NG = G // 512
PAIRS = 4
BANKS = 8


def tile_schur_complement_apply_h1_kernel(
    tc, lower, pivot_inv, u_words, u_scales, diag, guesses, out_0, out_1, out_2
):
    nc = tc.nc
    with ExitStack() as ctx:
        keep = ctx.enter_context(tc.tile_pool(name="keep", bufs=1))
        psum = ctx.enter_context(tc.psum_pool(name="psum", bufs=1))
        ctx.enter_context(tc.manual_schedule())

        free_banks = list(range(BANKS))

        def new_bank(shape):
            index = free_banks.pop(0)
            bank = psum.tile(shape, F32, name="bank%d" % index, tag="bank%d" % index)
            return bank, index

        def pair_rows(matrix, pair):
            group, half = divmod(pair, 2)
            rows = matrix[group * PASS : (group + 1) * PASS, :].rearrange("(p t) c -> p t c", t=4)
            return rows[:, 2 * half : 2 * half + 2, :]

        l_tiles = {}

        def load_lower(pair, g0, g1):
            t = keep.tile([P, 2, (g1 - g0) * PASS], BF16, name="l_%d_%d" % (pair, g0), align_bytes=64)
            nc.sync.dma_start(out=t[:], in_=pair_rows(lower, pair)[:, :, g0 * PASS : g1 * PASS])
            for g in range(g0, g1):
                l_tiles[pair, g] = (t, g - g0)

        u_tiles = {}

        def load_upper(h):
            t = keep.tile([P, NK, R], U8, name="u_%d" % h, align_bytes=64)
            nc.sync.dma_start(
                out=t[:].bitcast(I32),
                in_=u_words[:, :, 1024 * h : 1024 * (h + 1)].rearrange("g p n -> p g n").bitcast(I32),
            )
            u_tiles[h] = t

        d_tiles = {}

        def load_diag(pair):
            t = keep.tile([P, 2, R], BF16, name="d_%d" % pair, align_bytes=64)
            nc.sync.dma_start(out=t[:], in_=pair_rows(diag, pair))
            d_tiles[pair] = t

        x_tiles = {}

        def load_guesses(h, n0, n1):
            t = keep.tile([P, 4, 512 * (n1 - n0)], BF16, name="x_%d_%d" % (h, n0), align_bytes=64)
            rows = guesses[h * PASS : (h + 1) * PASS, 512 * n0 : 512 * n1]
            nc.sync.dma_start(out=t[:], in_=rows.rearrange("(p t) m -> p t m", t=4))
            for n in range(n0, n1):
                x_tiles[h, n] = t[:, :, 512 * (n - n0) : 512 * (n - n0 + 1)]

        ident = keep.tile([P, P], F32, name="ident")
        u_plane = keep.tile([P, NK, R], U8, name="u_plane", align_bytes=64)
        piv = keep.tile([P, NK, 2, 2], BF16, name="piv", align_bytes=64)
        neg_piv = keep.tile([P, NK, 2, 2], BF16, name="neg_piv", align_bytes=64)
        warm_bf = keep.tile([P, 1024], BF16, name="warm_bf", align_bytes=64)
        warm_codes = keep.tile([P, 256], U32, name="warm_codes", align_bytes=64)
        warm_plane = keep.tile([P, 256], U8, name="warm_plane", align_bytes=64)
        nc.gpsimd.memset(warm_bf[:].bitcast(I32), 0)
        nc.vector.memset(u_plane[:].rearrange("p g n -> p (g n)").bitcast(I32), 0)
        nc.vector.quantize_mx(out=warm_codes[:].bitcast(FP8X4), scales=warm_plane[:], in_=warm_bf[:])
        make_identity(nc, ident[:])
        load_lower(0, 0, 1)
        nc.sync.dma_start(
            out=piv[:].rearrange("p g u e -> p g (u e)"),
            in_=pivot_inv.rearrange("(g p t) -> p g t", g=NK, t=4),
        )
        load_lower(0, 1, 2)
        load_lower(0, 2, 4)
        for q in range(4):
            nc.sync.dma_start(
                out=u_plane[32 * q : 32 * q + 4, :, :].bitcast(I32),
                in_=u_scales[:, 4 * q : 4 * q + 4, :].rearrange("g r n -> r g n").bitcast(I32),
            )
        load_upper(0)
        load_lower(1, 0, 2)
        load_lower(1, 2, 4)
        load_upper(1)
        load_diag(0)
        load_guesses(0, 0, 1)
        load_lower(2, 0, 2)
        load_guesses(1, 0, 1)
        load_diag(1)
        load_lower(2, 2, 4)
        load_guesses(0, 1, 3)
        load_guesses(1, 1, 3)
        load_lower(3, 0, 2)
        load_diag(2)
        load_lower(3, 2, 4)
        load_diag(3)
        nc.vector.tensor_scalar(
            out=neg_piv[:].rearrange("p g u e -> p (g u e)"),
            in0=piv[:].rearrange("p g u e -> p (g u e)"),
            scalar1=-1.0,
            scalar2=None,
            op0=ALU.mult,
        )


        def warm(count):
            bank, index = new_bank([P, 256])
            free_banks.append(index)
            for i in range(count):
                nc.tensor.matmul_mx(
                    out=bank[:],
                    lhsT=warm_codes[:, :P].bitcast(FP8X4),
                    lhsT_scale=warm_plane[:, :P],
                    rhs=warm_codes[:].bitcast(FP8X4),
                    rhs_scale=warm_plane[:],
                    start=True,
                    stop=True,
                )

        lt_banks, f_bf, f_mx = {}, {}, {}

        l_sorted = {}

        def sort_lower(pair, g):
            t, i = l_tiles[pair, g]
            words = t[:].bitcast(F32)[:, :, 256 * i : 256 * (i + 1)]
            ls = keep.tile([P, 2, 2, P], F32, name="l_sorted", tag="l_sorted", bufs=4, align_bytes=64)
            nc.scalar.copy(out=ls[:], in_=words.rearrange("r j (p u) -> r j u p", u=2))
            l_sorted[pair, g] = ls

        def turn_lower(pair, g):
            t, i = l_tiles[pair, g]
            words = t[:].bitcast(F32)
            bank, index = new_bank([P, 2, 2, P])
            for j in range(2):
                for u in range(2):
                    if (pair, g) in l_sorted:
                        src = l_sorted[pair, g][:, j, u, :]
                    else:
                        src = words[:, j, 256 * i + u : 256 * (i + 1) : 2]
                    nc.tensor.transpose(bank[:, u, j, :], src, ident[:])
            lt_banks[pair, g] = bank, index

        def scale_lower(pair, g):
            if g % 2 == 0:
                f_bf[pair, g // 2] = keep.tile(
                    [P, 2, 2 * P, 2, 2], BF16, name="f_bf", tag="f_bf", bufs=2, align_bytes=64
                )
            fb = f_bf[pair, g // 2][:, g % 2]
            bank, index = lt_banks[pair, g]
            free_banks.append(index)
            src = bank[:].rearrange("p u j r -> p u (j r)").bitcast(BF16)
            nc.vector.tensor_tensor(
                out=fb,
                in0=src.rearrange("p u (n e) -> p n u e", e=2),
                in1=neg_piv[:, g : g + 1, :, :].to_broadcast([P, 2 * P, 2, 2]),
                op=ALU.mult,
            )

        def quantize(src, width, name, bufs):
            codes = keep.tile([P, width], U32, name=name + "_codes", tag=name + "_codes", bufs=bufs, align_bytes=64)
            plane = keep.tile([P, width], U8, name=name + "_plane", tag=name + "_plane", bufs=bufs, align_bytes=64)
            nc.vector.quantize_mx(out=codes[:].bitcast(FP8X4), scales=plane[:], in_=src)
            return codes, plane

        f_codes = {}

        def quantize_f(pair, g0, g1):
            if g0 % 2 == 0:
                codes = keep.tile([P, 2, 2 * P], U32, name="f_codes", tag="f_codes", bufs=4, align_bytes=64)
                plane = keep.tile([P, 2, 2 * P], U8, name="f_plane", tag="f_plane", bufs=4, align_bytes=64)
                f_codes[pair, g0 // 2] = codes, plane
            codes, plane = f_codes[pair, g0 // 2]
            part = slice(g0 % 2, g0 % 2 + g1 - g0)
            nc.vector.quantize_mx(
                out=codes[:, part].rearrange("p g n -> p (g n)").bitcast(FP8X4),
                scales=plane[:, part].rearrange("p g n -> p (g n)"),
                in_=f_bf[pair, g0 // 2][:, part].rearrange("p g n u e -> p (g n u e)"),
            )
            for g in range(g0, g1):
                f_mx[pair, g] = codes[:, g % 2], plane[:, g % 2]

        s_banks, s_bf, st_banks, st_bf, s_mx = {}, {}, {}, {}, {}

        def first_product(pair, halves, passes, by_tile=False):
            steps = [(g, j) for g in passes for j in range(2)]
            if by_tile:
                steps = [(g, j) for j in range(2) for g in passes]
            for g, j in steps:
                codes, plane = f_mx[pair, g]
                for h in halves:
                    if True:
                        if g == 0:
                            s_banks[pair, h, j] = new_bank([P, 512])
                        nc.tensor.matmul_mx(
                            out=s_banks[pair, h, j][0][:],
                            lhsT=codes[:, j * P : (j + 1) * P].bitcast(FP8X4),
                            lhsT_scale=plane[:, j * P : (j + 1) * P],
                            rhs=u_tiles[h][:, g, :].bitcast(FP4X4),
                            rhs_scale=u_plane[:, g, 512 * h : 512 * (h + 1)],
                            start=(g == 0),
                            stop=(g == NK - 1),
                        )

        def add_diag(pair, h, j):
            sb = keep.tile([P, 2, P, 2], BF16, name="s_bf", tag="s_bf", bufs=6, align_bytes=64)
            bank, index = s_banks[pair, h, j]
            free_banks.append(index)
            nc.vector.tensor_tensor(
                out=sb[:],
                in0=bank[:].rearrange("r (p u e) -> r u p e", u=2, e=2),
                in1=d_tiles[pair][:, j, 512 * h : 512 * (h + 1)].rearrange("r (p u e) -> r u p e", u=2, e=2),
                op=ALU.add,
            )
            s_bf[pair, h, j] = sb

        def turn_s(pair, h):
            bank, index = new_bank([P, 2, 2, P])
            for j in range(2):
                words = s_bf[pair, h, j][:].rearrange("r u p e -> r (u p e)").bitcast(F32)
                for u in range(2):
                    nc.tensor.transpose(bank[:, u, j, :], words[:, u * P : (u + 1) * P], ident[:])
            st_banks[pair, h] = bank, index

        def copy_s(pair, h, copy=nc.scalar.copy):
            stb = keep.tile([P, 2 * P, 4], BF16, name="st_bf", tag="st_bf", bufs=2, align_bytes=64)
            bank, index = st_banks[pair, h]
            free_banks.append(index)
            copy(out=stb[:].bitcast(F32), in_=bank[:].rearrange("p u j r -> p (j r) u"))
            st_bf[pair, h] = stb

        def quantize_s(pair, h):
            s_mx[pair, h] = quantize(st_bf[pair, h][:].rearrange("p n t -> p (n t)"), 2 * P, "s", 8)

        def interleave(copy, dst, src):
            copy(
                out=dst.rearrange("p (c i) t -> p c t i", i=4),
                in_=src.rearrange("p t (c i) -> p c t i", i=4),
            )

        x_bf, x_mx = {}, {}

        def group_x(h, n):
            xb = keep.tile([P, 512, 4], BF16, name="x_bf", tag="x_bf", bufs=3, align_bytes=64)
            for m0 in range(0, 512, 256):
                interleave(nc.scalar.copy, xb[:, m0 : m0 + 256, :], x_tiles[h, n][:, :, m0 : m0 + 256])
            x_bf[h, n] = xb

        def quantize_x(h, n):
            x_mx[h, n] = quantize(x_bf[h, n][:].rearrange("p m t -> p (m t)"), 512, "x", 6)

        y_banks, y_f32, y_bf = {}, {}, {}
        y_planes, y_codes = {}, {}

        def second_product(pair, n):
            for h in range(NC):
                s_codes, s_plane = s_mx[pair, h]
                x_codes, x_plane = x_mx[h, n]
                for j in range(2):
                    if h == 0:
                        y_banks[pair, n, j] = new_bank([P, 512])
                    nc.tensor.matmul_mx(
                        out=y_banks[pair, n, j][0][:],
                        lhsT=s_codes[:, j * P : (j + 1) * P].bitcast(FP8X4),
                        lhsT_scale=s_plane[:, j * P : (j + 1) * P],
                        rhs=x_codes[:].bitcast(FP8X4),
                        rhs_scale=x_plane[:],
                        start=(h == 0),
                        stop=(h == NC - 1),
                    )

        def copy_y(pair, n, copies=(nc.scalar.copy, nc.scalar.copy)):
            group, half = divmod(pair, 2)
            if half == 0:
                y_f32[group, n] = keep.tile([P, 4, 512], F32, name="y_%d_%d" % (group, n), align_bytes=64)
            yt = y_f32[group, n]
            for j in range(2):
                bank, index = y_banks[pair, n, j]
                free_banks.append(index)
                copies[j](out=yt[:, 2 * half + j, :], in_=bank[:])
            nc.sync.dma_start(
                out=pair_rows(out_0, pair)[:, :, 512 * n : 512 * (n + 1)], in_=yt[:, 2 * half : 2 * half + 2, :]
            )

        def group_y(group, n, split=512):
            yb = keep.tile([P, 512, 4], BF16, name="y_bf", tag="y_bf", bufs=2, align_bytes=64)
            src = y_f32[group, n]
            if split > 0:
                interleave(nc.vector.tensor_copy, yb[:, :split, :], src[:, :, :split])
            for m0 in range(split, 512, 256):
                m1 = min(m0 + 256, 512)
                interleave(nc.scalar.copy, yb[:, m0:m1, :], src[:, :, m0:m1])
            y_bf[group, n] = yb

        def quantize_y(group, n):
            if n == 0:
                y_planes[group] = keep.tile([P, G], U8, name="y_plane_%d" % group, align_bytes=64)
            plane = y_planes[group]
            codes = keep.tile([P, 512], U32, name="y_codes_%d_%d" % (group, n), align_bytes=64)
            nc.vector.quantize_mx(
                out=codes[:].bitcast(FP8X4),
                scales=plane[:, 512 * n : 512 * (n + 1)],
                in_=y_bf[group, n][:].rearrange("p m t -> p (m t)"),
            )
            y_codes[group, n] = codes

        def store_planes(group, n):
            plane = y_planes[group]
            nc.sync.dma_start(
                out=out_1[group, :, 512 * n : 512 * (n + 1), :].rearrange("p m t -> p (m t)").bitcast(I32),
                in_=y_codes[group, n][:].bitcast(I32),
            )
            if n == NG - 1:
                for q in range(4):
                    queue = nc.sync if q % 2 == 0 or group == 0 else nc.scalar
                    queue.dma_start(
                        out=out_2[group, 4 * q : 4 * q + 4, :].bitcast(I32),
                        in_=plane[32 * q : 32 * q + 4, :].bitcast(I32),
                    )

        def make_f(pair, g0):
            scale_lower(pair, g0)
            scale_lower(pair, g0 + 1)

        def product_y(*units):
            for unit in units:
                second_product(*unit)
                copy_y(*unit)

        def add_half(pair, h):
            add_diag(pair, h, 0)
            add_diag(pair, h, 1)

        warm(8)
        turn_lower(0, 0)
        scale_lower(0, 0)
        turn_lower(0, 1)
        scale_lower(0, 1)
        quantize_f(0, 0, 1)
        warm(4)
        turn_lower(0, 2)
        turn_lower(0, 3)
        quantize_f(0, 1, 2)
        make_f(0, 2)
        quantize_f(0, 2, 3)
        quantize_f(0, 3, 4)
        for g in range(NK):
            sort_lower(1, g)
        first_product(0, (0,), range(NK))
        for g in range(NK):
            turn_lower(1, g)
        make_f(1, 0)
        scale_lower(1, 2)
        quantize_f(1, 0, 2)
        scale_lower(1, 3)
        group_x(0, 0)
        sort_lower(2, 0)
        sort_lower(2, 1)
        group_x(1, 0)
        first_product(0, (1,), range(NK))
        add_diag(0, 0, 0)
        quantize_f(1, 2, 4)
        add_diag(0, 0, 1)
        add_half(0, 1)
        quantize_x(0, 0)
        first_product(1, (0,), range(NK))
        turn_s(0, 0)
        turn_s(0, 1)
        turn_lower(2, 0)
        turn_lower(2, 1)
        copy_s(0, 0)
        copy_s(0, 1)
        group_x(0, 1)
        add_half(1, 0)
        make_f(2, 0)
        quantize_s(0, 0)
        quantize_f(2, 0, 2)
        quantize_s(0, 1)
        quantize_x(1, 0)
        first_product(1, (1,), range(NK))
        turn_s(1, 0)
        turn_lower(2, 2)
        turn_lower(2, 3)
        copy_s(1, 0)
        group_x(1, 1)
        make_f(2, 2)
        add_diag(1, 1, 0)
        quantize_f(2, 2, 4)
        add_diag(1, 1, 1)
        quantize_s(1, 0)
        product_y((0, 0))
        quantize_x(0, 1)
        first_product(2, (0,), range(NK))
        turn_s(1, 1)
        turn_lower(3, 0)
        turn_lower(3, 1)
        copy_s(1, 1)
        quantize_x(1, 1)
        group_x(0, 2)
        add_half(2, 0)
        quantize_s(1, 1)
        make_f(3, 0)
        product_y((0, 1))
        quantize_f(3, 0, 2)
        quantize_x(0, 2)
        first_product(2, (1,), range(NK))
        turn_s(2, 0)
        turn_lower(3, 2)
        turn_lower(3, 3)
        copy_s(2, 0)
        group_x(1, 2)
        add_diag(2, 1, 0)
        make_f(3, 2)
        add_diag(2, 1, 1)
        quantize_f(3, 2, 4)
        product_y((1, 0), (1, 1))
        quantize_s(2, 0)
        quantize_x(1, 2)
        group_y(0, 0, 512)
        first_product(3, (0,), range(NK))
        turn_s(2, 1)
        copy_s(2, 1)
        group_y(0, 1, 512)
        add_half(3, 0)
        quantize_y(0, 0)
        quantize_s(2, 1)
        store_planes(0, 0)
        product_y((0, 2), (1, 2))
        quantize_y(0, 1)
        store_planes(0, 1)
        first_product(3, (1,), range(NK), by_tile=True)
        group_y(0, 2, 256)
        turn_s(3, 0)
        add_half(3, 1)
        copy_s(3, 0)
        quantize_y(0, 2)
        quantize_s(3, 0)
        second_product(2, 0)
        turn_s(3, 1)
        store_planes(0, 2)
        copy_y(2, 0)
        copy_s(3, 1, nc.vector.tensor_copy)
        quantize_s(3, 1)
        second_product(2, 1)
        copy_y(2, 1, (nc.scalar.copy, nc.vector.tensor_copy))
        product_y((3, 0))
        group_y(1, 0)
        product_y((3, 1))
        group_y(1, 1)
        quantize_y(1, 0)
        product_y((2, 2))
        second_product(3, 2)
        quantize_y(1, 1)
        store_planes(1, 0)
        copy_y(3, 2, (nc.scalar.copy, nc.scalar.copy))
        store_planes(1, 1)
        group_y(1, 2, 320)
        quantize_y(1, 2)
        store_planes(1, 2)
